import numpy as np
import ml_dtypes


def mxq(x, axis, fmt="e4m3"):
    dtype, down = {"e4m3": (ml_dtypes.float8_e4m3fn, 7), "e5m2": (ml_dtypes.float8_e5m2, 14)}[fmt]
    v = np.moveaxis(np.asarray(x, np.float32).astype(ml_dtypes.bfloat16).astype(np.float64), axis, -1)
    blocks = v.reshape(v.shape[:-1] + (-1, 32))
    amax = np.abs(blocks).max(-1, keepdims=True)
    byte = np.maximum(np.where(amax > 0, np.frexp(amax)[1] - 1 + 127, 0) - down, 1)
    scale = np.exp2(byte - 127.0)
    codes = (blocks / scale).astype(np.float32).astype(dtype).astype(np.float64)
    return np.moveaxis((codes * scale).reshape(v.shape), -1, axis)


WIDE = False


def mx_kscale(k):
    if not WIDE:
        return np.ones(k)
    levels = np.array([10, -10, 5, -5, 0])
    if k % 512:
        return np.exp2(np.random.permutation(np.resize(levels, k // 32))).repeat(32)
    a = np.empty((k // 512, 16))
    for p in range(k // 512):
        a[p, :8] = np.random.permutation(np.resize(levels, 8))
        for g in range(8):
            far = levels[np.abs(levels - a[p, g]) >= 10]
            a[p, g + 8] = far[np.random.randint(len(far))]
    return np.exp2(a.ravel()).repeat(32)


def f64(x):
    return np.asarray(x).astype(np.float64)


def striped(idx):
    return np.tile(idx.reshape(-1, 16).T, (8, 1)).astype(np.uint16)


def unstriped(offs):
    return offs[:16].T.reshape(-1).astype(np.int64)


def striped8(idx):
    return np.concatenate([x.reshape(-1, 16).T for x in idx]).astype(np.uint16)


def runs(offs, k):
    lists = np.stack([offs[16 * r : 16 * r + 16].T.reshape(-1) for r in range(8)]).astype(np.int64)
    return lists[np.arange(k) % 512 // 64]


def pack_weight(w):
    k, n = w.shape
    w = f64(np.asarray(w, np.float32).astype(ml_dtypes.bfloat16)).reshape(k // 32, 32, n)
    amax = np.abs(w).max(1)
    byte = np.clip(np.where(amax > 0, np.frexp(amax)[1] - 1 + 127 - 7, 1), 1, 254)
    scaled = (w * np.exp2(127.0 - byte)[:, None, :]).reshape(k, n).astype(np.float32)
    words = np.ascontiguousarray(scaled.reshape(k // 512, 128, 4, n).transpose(0, 1, 3, 2)).astype(ml_dtypes.float8_e4m3fn).view(np.uint8)
    return words, np.ascontiguousarray(byte.astype(np.uint8).reshape(k // 512, 16, n))


def unpack_weight(words, scales):
    g, p, n, _ = words.shape
    vals = np.ascontiguousarray(words).view(ml_dtypes.float8_e4m3fn).astype(np.float64) * np.repeat(np.exp2(scales.astype(np.float64) - 127.0), 8, axis=1)[..., None]
    return vals.transpose(0, 1, 3, 2).reshape(g * 512, n)


def sigmoid(v):
    return 1.0 / (1.0 + np.exp(-np.maximum(v, -700.0)))

def planes(y):
    n, m = y.shape
    v = y.astype(np.float32).astype(ml_dtypes.bfloat16).astype(np.float64).reshape(n // 32, 32, m)
    top = np.abs(v).max(1)
    byte = np.clip(np.where(top > 0, np.frexp(top)[1] - 1 + 127 - 7, 1), 1, 254)
    codes = (v * np.exp2(127.0 - byte)[:, None, :]).reshape(n, m).astype(np.float32).astype(ml_dtypes.float8_e4m3fn).view(np.uint8)
    words = codes.reshape(n // 512, 128, 4, m).transpose(0, 1, 3, 2)
    return np.ascontiguousarray(words), np.ascontiguousarray(byte.astype(np.uint8).reshape(n // 512, 16, m))


K, T, S, V, H, W = 512, 2048, 512, 256, 512, 1024


def setup_inputs():
    n = np.random.standard_normal
    s = mx_kscale(K)[:, None]
    u = mx_kscale(S)
    packed_xT = pack_weight(n((K, T)) * s)
    packed_w1 = pack_weight(n((K, H)) / np.sqrt(K) / s)
    packed_w2 = pack_weight(n((K, H)) / np.sqrt(K) / s)
    packed_w3 = pack_weight(n((K, H)) / np.sqrt(K) / s)
    return {
        "x_words": packed_xT[0],
        "x_scales": packed_xT[1],
        "w1_words": packed_w1[0],
        "w1_scales": packed_w1[1],
        "w2_words": packed_w2[0],
        "w2_scales": packed_w2[1],
        "sl": np.random.uniform(1.0, 2.0, (H, 1)).astype(np.float32),
        "th": (0.5 * n((H, 1))).astype(np.float32),
        "w3_words": packed_w3[0],
        "w3_scales": packed_w3[1],
        "tau": np.random.uniform(0.3, 0.9, (H, 1)).astype(np.float32),
        "tau2": np.random.uniform(0.3, 0.9, (H, 1)).astype(np.float32),
        "ga": (np.random.uniform(0.5, 1.5, (H, 1)) * u[:, None]).astype(np.float32),
        "gb": (np.random.uniform(0.5, 1.5, (H, 1)) / u[:, None]).astype(np.float32),
        "tau3": np.random.uniform(0.3, 0.9, (S, 1)).astype(np.float32),
        "offs": striped(np.random.permutation(T)[:S]),
        "two": striped(np.random.permutation(T)[:S]),
        "n1": striped8(np.stack([np.random.permutation(S) for _ in range(8)])),
        "n2": striped8(np.stack([np.random.permutation(S) for _ in range(8)])),
        "three": striped(np.random.permutation(T)[:V]),
        "n3": striped8(np.stack([np.random.permutation(V) for _ in range(8)])),
        "n4": striped8(np.stack([np.random.permutation(V) for _ in range(8)])),
        "n5": striped(np.random.randint(0, V, W)),
    }


def reference(x_words, x_scales, w1_words, w1_scales, w2_words, w2_scales, sl, th, w3_words, w3_scales, tau, tau2, ga, gb, tau3, offs, two, n1, n2, three, n3, n4, n5):
    xq = unpack_weight(x_words, x_scales)[:, unstriped(offs)]
    y = unpack_weight(w1_words, w1_scales).T @ xq
    x_two = unpack_weight(x_words, x_scales)[:, unstriped(two)]
    d = unpack_weight(w2_words, w2_scales).T @ x_two
    sg = sigmoid(f64(sl) * (d[np.arange(H)[:, None], runs(n1, H)] - f64(th)))
    z = f64(ga) * (y * sg - (0.5 * (y[np.arange(H)[:, None], runs(n2, H)])))
    x_three = unpack_weight(x_words, x_scales)[:, unstriped(three)]
    b = unpack_weight(w3_words, w3_scales).T @ x_three
    top = b.max(axis=1, keepdims=True)
    ea = np.exp(f64(tau) * (b[np.arange(H)[:, None], runs(n3, H)] - top))
    low = b.min(axis=1, keepdims=True)
    ea2 = np.exp(f64(tau2) * (low - (b[np.arange(H)[:, None], runs(n4, H)])))
    z2 = f64(gb) * (1.5 * (b * (ea + ea2)))
    s = 0.0625 * ((mxq(z, 0, "e4m3").T @ mxq(z2, 0, "e4m3")))
    top2 = s.max(axis=1, keepdims=True)
    ea3 = np.exp(f64(tau3) * (s[:, unstriped(n5)] - top2))
    ms = ea3.reshape(S, V, 4).sum(axis=2)
    out_0 = (1.5 * s) / (ms + 0.5)
    return (out_0,) + planes(out_0)

@@ -1,0 +1,254 @@
+from contextlib import ExitStack
+
+import concourse.mybir as mybir
+
+F32 = mybir.dt.float32
+BF16 = mybir.dt.bfloat16
+U32 = mybir.dt.uint32
+I32 = mybir.dt.int32
+U16 = mybir.dt.uint16
+U8 = mybir.dt.uint8
+FP8X4 = mybir.dt.float8_e4m3fn_x4
+ALU = mybir.AluOpType
+ACT = mybir.ActivationFunctionType
+AXIS = mybir.AxisListType
+
+P = 128
+PACK = 4
+T, S, V, H = 2048, 512, 256, 512
+MEMBERS = 4
+FLOPS = 2 * 512 * (H * S + H * S + H * V + S * V)
+
+
+def tile_picked_twkgxbedfegs_none_po_kernel(
+    tc, x_words, x_scales, w1_words, w1_scales, w2_words, w2_scales, sl, th, w3_words, w3_scales,
+    tau, tau2, ga, gb, tau3, offs, two, n1, n2, three, n3, n4, n5, out_0, out_1, out_2,
+):
+    nc = tc.nc
+    with ExitStack() as ctx:
+        lists = ctx.enter_context(tc.tile_pool(name="lists", bufs=1))
+        keep = ctx.enter_context(tc.tile_pool(name="keep", bufs=1))
+        psum = ctx.enter_context(tc.psum_pool(name="psum", bufs=1))
+
+        def sb(name, shape, dtype, tag=None):
+            return keep.tile(shape, dtype, name=name, tag=tag or name, align_bytes=64)
+
+        def load_list(name, src):
+            tile = lists.tile(list(src.shape), U16, name=name)
+            nc.sync.dma_start(tile[:], src)
+            return tile
+
+        def load_words(name, src):
+            tile = sb(name, [P, src.shape[2]], U32)
+            nc.sync.dma_start(tile[:].bitcast(I32), src[0].rearrange("p c r -> p (c r)").bitcast(I32))
+            return tile
+
+        def load_scales(name, src, zero_engine, queue):
+            tile = sb(name, [P, src.shape[2]], U8)
+            zero_engine.memset(tile[:].bitcast(I32), 0)
+            for q in range(4):
+                queue.dma_start(tile[32 * q : 32 * q + 4, :].bitcast(I32), src[0, 4 * q : 4 * q + 4, :].bitcast(I32))
+            return tile
+
+        def load_column(name, src, queue):
+            tile = sb(name, [P, PACK], F32)
+            queue.dma_start(tile[:], src.rearrange("(p t) o -> p (t o)", t=PACK))
+            return tile
+
+        xs = load_scales("xs", x_scales, nc.vector, nc.scalar)
+        w2s_raw = load_scales("w2s_raw", w2_scales, nc.vector, nc.scalar)
+        two_l = load_list("two_l", two)
+        offs_l = load_list("offs_l", offs)
+        xw = load_words("xw", x_words)
+        w2w_raw = load_words("w2w_raw", w2_words)
+        sl_c = load_column("sl_c", sl, nc.sync)
+        th_c = load_column("th_c", th, nc.sync)
+        n1_l = load_list("n1_l", n1)
+        w1s_raw = load_scales("w1s_raw", w1_scales, nc.gpsimd, nc.gpsimd)
+        w1w_raw = load_words("w1w_raw", w1_words)
+        ga_c = load_column("ga_c", ga, nc.sync)
+        n2_l = load_list("n2_l", n2)
+        three_l = load_list("three_l", three)
+        w3s_raw = load_scales("w3s_raw", w3_scales, nc.gpsimd, nc.gpsimd)
+        w3w_raw = load_words("w3w_raw", w3_words)
+        gb_c = load_column("gb_c", gb, nc.sync)
+        tau_c = load_column("tau_c", tau, nc.sync)
+        tau2_c = load_column("tau2_c", tau2, nc.sync)
+        n3_l = load_list("n3_l", n3)
+        n4_l = load_list("n4_l", n4)
+        tau3_c = load_column("tau3_c", tau3, nc.sync)
+        n5_l = load_list("n5_l", n5)
+
+        def gather(name, window, offsets, dtype, tag=None):
+            tile = sb(name, [P, offsets.shape[1] * 16], dtype, tag)
+            nc.vector.tensor_copy(tile[:], window[:].indirect(offsets[:]))
+            return tile
+
+        def deal(name, raw, dtype, copy):
+            tile = sb(name, [P, H], dtype)
+            copy(tile[:].rearrange("p (t m) -> p m t", t=PACK), raw[:].rearrange("p (m t) -> p m t", t=PACK))
+            return tile
+
+        def products(tag, words, scales, x_w, x_s):
+            banks = []
+            for t in range(PACK):
+                bank = psum.tile([P, x_w.shape[1]], F32, name="%s%d" % (tag, t), tag="%s%d" % (tag, t))
+                cols = slice(t * P, (t + 1) * P)
+                nc.tensor.matmul_mx(
+                    out=bank[:], lhsT=words[:, cols].bitcast(FP8X4), lhsT_scale=scales[:, cols],
+                    rhs=x_w[:].bitcast(FP8X4), rhs_scale=x_s[:], start=True, stop=True,
+                )
+                banks.append(bank)
+            return banks
+
+        x2s = gather("x2s", xs, two_l, U8)
+        w2w = deal("w2w", w2w_raw, U32, nc.scalar.copy)
+        x1s = gather("x1s", xs, offs_l, U8)
+        w2s = deal("w2s", w2s_raw, U8, nc.vector.tensor_copy)
+        x2w = gather("x2w", xw, two_l, U32, "w2s_raw")
+        sg_bias = sb("sg_bias", [P, PACK], F32)
+        nc.vector.scalar_tensor_tensor(sg_bias[:], sl_c[:], -1.0, th_c[:], ALU.mult, ALU.mult)
+        d_banks = products("pa", w2w, w2s, x2w, x2s)
+
+        w1w = deal("w1w", w1w_raw, U32, nc.scalar.copy)
+        w3w = deal("w3w", w3w_raw, U32, nc.scalar.copy)
+
+        s_win = [sb("s_win%d" % t, [P, 1024], F32) for t in range(PACK)]
+        sg = [s_win[t][:, V : V + S] for t in range(PACK)]
+        ea = [s_win[t][:, V + S :] for t in range(PACK)]
+        d_win = [sb("d_win%d" % t, [P, S], F32) for t in range(PACK)]
+
+        def sigmoid_of(t):
+            for h in range(2):
+                nc.scalar.activation(
+                    sg[t][:, h * 256 : (h + 1) * 256], d_win[t][:].indirect(n1_l[:, h * 16 : (h + 1) * 16]),
+                    ACT.Sigmoid, bias=sg_bias[:, t : t + 1], scale=sl_c[:, t : t + 1],
+                )
+
+        nc.vector.tensor_copy(d_win[0][:], d_banks[0][:])
+        sigmoid_of(0)
+        nc.vector.tensor_copy(d_win[1][:], d_banks[1][:])
+        sigmoid_of(1)
+        x1w = gather("x1w", xw, offs_l, U32)
+        w1s = deal("w1s", w1s_raw, U8, nc.vector.tensor_copy)
+        for t in (2, 3):
+            nc.vector.tensor_copy(d_win[t][:], d_banks[t][:])
+            sigmoid_of(t)
+
+        y_banks = products("pb", w1w, w1s, x1w, x1s)
+        y_win = [sb("y_win%d" % t, [P, S], F32) for t in range(PACK)]
+        fetched = sb("fetched", [P, PACK, S], F32)
+        gated = sb("gated", [P, PACK, S], F32)
+        for t in range(PACK):
+            nc.vector.tensor_scalar(y_win[t][:], y_banks[t][:], ga_c[:, t : t + 1], None, ALU.mult)
+            for h in range(2):
+                nc.scalar.activation(
+                    fetched[:, t, h * 256 : (h + 1) * 256], y_win[t][:].indirect(n2_l[:, h * 16 : (h + 1) * 16]), ACT.Copy, scale=-0.5,
+                )
+
+        x3s = gather("x3s", xs, three_l, U8)
+        x3w = gather("x3w", xw, three_l, U32)
+        w3s = deal("w3s", w3s_raw, U8, nc.vector.tensor_copy)
+        b_banks = products("pa", w3w, w3s, x3w, x3s)
+        gb15 = sb("gb15", [P, PACK], F32)
+        nc.vector.tensor_scalar(gb15[:], gb_c[:], 1.5, None, ALU.mult)
+        neg_tau2 = sb("neg_tau2", [P, PACK], F32)
+        nc.vector.tensor_scalar(neg_tau2[:], tau2_c[:], -1.0, None, ALU.mult)
+        b_win = [sb("b_win%d" % t, [P, 2 * V], F32) for t in range(PACK)]
+        top = sb("top", [P, PACK], F32)
+        low = sb("low", [P, PACK], F32)
+        weighted_b = sb("weighted_b", [P, PACK, V], F32)
+        for t in range(PACK):
+            nc.vector.tensor_scalar(b_win[t][:, :V], b_banks[t][:], 1.0, None, ALU.mult, ALU.max, accum_out=top[:, t : t + 1])
+            nc.vector.tensor_scalar(b_win[t][:, V:], b_banks[t][:], 1.0, None, ALU.mult, ALU.min, accum_out=low[:, t : t + 1])
+        ea_bias = sb("ea_bias", [P, PACK], F32)
+        nc.vector.scalar_tensor_tensor(ea_bias[:], top[:], -1.0, tau_c[:], ALU.mult, ALU.mult)
+        ea2_bias = sb("ea2_bias", [P, PACK], F32)
+        nc.vector.tensor_tensor(ea2_bias[:], low[:], tau2_c[:], ALU.mult)
+        for t in range(PACK):
+            nc.vector.tensor_scalar(weighted_b[:, t, :], b_win[t][:, V:], gb15[:, t : t + 1], None, ALU.mult)
+
+        for t in range(PACK):
+            nc.vector.tensor_tensor(gated[:, t, :], y_win[t][:], sg[t], ALU.mult)
+        z_bf = sb("z_bf", [P, S * PACK], BF16)
+        nc.vector.tensor_tensor(
+            z_bf[:].rearrange("p (u m t) -> p m t u", u=PACK, t=PACK),
+            gated[:].rearrange("p t (m u) -> p m t u", u=PACK),
+            fetched[:].rearrange("p t (m u) -> p m t u", u=PACK),
+            ALU.add,
+        )
+        z_w = sb("z_w", [P, S], U32)
+        z_s = sb("z_s", [P, S], U8)
+        nc.vector.quantize_mx(out=z_w[:].bitcast(FP8X4), scales=z_s[:], in_=z_bf[:])
+
+        ea2 = sb("ea2", [P, PACK, V], F32)
+        both = sb("both", [P, PACK, V], F32)
+        for t in range(PACK):
+            nc.scalar.activation(
+                ea[t], b_win[t][:].indirect(n3_l[:]), ACT.Exp, bias=ea_bias[:, t : t + 1], scale=tau_c[:, t : t + 1],
+            )
+            nc.scalar.activation(
+                ea2[:, t, :], b_win[t][:].indirect(n4_l[:]), ACT.Exp, bias=ea2_bias[:, t : t + 1], scale=neg_tau2[:, t : t + 1],
+            )
+            nc.vector.tensor_tensor(both[:, t, :], ea[t], ea2[:, t, :], ALU.add)
+        z2_bf = sb("z2_bf", [P, V * PACK], BF16)
+        nc.vector.tensor_tensor(
+            z2_bf[:].rearrange("p (c i t) -> p c t i", i=4, t=PACK),
+            both[:].rearrange("p t (c i) -> p c t i", i=4),
+            weighted_b[:].rearrange("p t (c i) -> p c t i", i=4),
+            ALU.mult,
+        )
+        z2_w = sb("z2_w", [P, V], U32)
+        z2_s = sb("z2_s", [P, V], U8)
+        nc.vector.quantize_mx(out=z2_w[:].bitcast(FP8X4), scales=z2_s[:], in_=z2_bf[:])
+
+        s_banks = products("pb", z_w, z_s, z2_w, z2_s)
+        top2 = sb("top2", [P, PACK], F32)
+        ea3_bias = sb("ea3_bias", [P, PACK], F32)
+        for t in range(PACK):
+            nc.vector.tensor_scalar(s_win[t][:, :V], s_banks[t][:], 0.0625, None, ALU.mult, ALU.max, accum_out=top2[:, t : t + 1])
+            nc.vector.scalar_tensor_tensor(ea3_bias[:, t : t + 1], top2[:, t : t + 1], -1.0, tau3_c[:, t : t + 1], ALU.mult, ALU.mult)
+
+        out_rows = out_0.rearrange("(p t) v -> p t v", t=PACK)
+        out_w = sb("out_w", [P, V], U32)
+        out_s = sb("out_s", [P, V], U8)
+        CH = 128
+        for c in range(V // CH):
+            cols = slice(c * CH, (c + 1) * CH)
+            ea3 = sb("ea3_%d" % c, [P, PACK, CH, MEMBERS], F32)
+            pairs = sb("pairs_%d" % c, [P, PACK, CH, 2], F32)
+            den = sb("den_%d" % c, [P, PACK, CH], F32)
+            num = sb("num_%d" % c, [P, PACK, CH], F32)
+            for t in range(PACK):
+                nc.scalar.activation(
+                    ea3[:, t].rearrange("p v d -> p (v d)"),
+                    s_win[t][:].indirect(n5_l[:, c * CH // 4 : (c + 1) * CH // 4]),
+                    ACT.Exp, bias=ea3_bias[:, t : t + 1], scale=tau3_c[:, t : t + 1],
+                )
+                nc.vector.tensor_tensor(pairs[:, t], ea3[:, t, :, 0:2], ea3[:, t, :, 2:4], ALU.add)
+                nc.vector.scalar_tensor_tensor(den[:, t, :], pairs[:, t, :, 0], 0.5, pairs[:, t, :, 1], ALU.add, ALU.add)
+            prod2 = sb("prod2_%d" % c, [P, 2, CH], F32)
+            nc.vector.tensor_tensor(prod2[:], den[:, 0:2, :], den[:, 2:4, :], ALU.mult)
+            prod4 = sb("prod4_%d" % c, [P, CH], F32)
+            nc.vector.tensor_tensor(prod4[:], prod2[:, 0, :], prod2[:, 1, :], ALU.mult)
+            inv4 = sb("inv4_%d" % c, [P, CH], F32)
+            nc.vector.reciprocal(inv4[:], prod4[:])
+            for t in range(PACK):
+                nc.vector.tensor_tensor(num[:, t, :], s_win[t][:, cols], den[:, (t + 2) % PACK, :], ALU.mult)
+            inv2 = sb("inv2_%d" % c, [P, 2, CH], F32)
+            for j in range(2):
+                nc.vector.scalar_tensor_tensor(inv2[:, j, :], inv4[:], 1.5, prod2[:, 1 - j, :], ALU.mult, ALU.mult)
+            res = sb("res_%d" % c, [P, PACK, CH], F32)
+            for j in range(2):
+                nc.vector.tensor_tensor(res[:, 2 * j : 2 * j + 2, :], num[:, 2 * j : 2 * j + 2, :], inv2[:], ALU.mult)
+            nc.sync.dma_start(out_rows[:, :, cols], res[:])
+            res_bf = sb("res_bf_%d" % c, [P, CH * PACK], BF16)
+            nc.vector.tensor_copy(
+                res_bf[:].rearrange("p (c i t) -> p c t i", i=4, t=PACK),
+                res[:].rearrange("p t (c i) -> p c t i", i=4),
+            )
+            nc.vector.quantize_mx(out=out_w[:, cols].bitcast(FP8X4), scales=out_s[:, cols], in_=res_bf[:])
+        nc.sync.dma_start(out_1[0].rearrange("p c r -> p (c r)").bitcast(I32), out_w[:].bitcast(I32))
+        for q in range(4):
+            queue = nc.scalar if q % 2 else nc.sync
+            queue.dma_start(out_2[0, 4 * q : 4 * q + 4, :].bitcast(I32), out_s[32 * q : 32 * q + 4, :].bitcast(I32))

@@ -38,42 +38,49 @@ def tile_picked_twkgxbedfegs_none_po_kernel(
             nc.sync.dma_start(tile[:], src)
             return tile
 
-        def load_words(name, src):
+        def load_words(name, src, queue=nc.sync):
             tile = sb(name, [P, src.shape[2]], U32)
-            nc.sync.dma_start(tile[:].bitcast(I32), src[0].rearrange("p c r -> p (c r)").bitcast(I32))
+            queue.dma_start(tile[:].bitcast(I32), src[0].rearrange("p c r -> p (c r)").bitcast(I32))
             return tile
 
-        def load_scales(name, src, zero_engine, queue):
-            tile = sb(name, [P, src.shape[2]], U8)
-            zero_engine.memset(tile[:].bitcast(I32), 0)
-            for q in range(4):
-                queue.dma_start(tile[32 * q : 32 * q + 4, :].bitcast(I32), src[0, 4 * q : 4 * q + 4, :].bitcast(I32))
+        def zeroed_plane(name, width):
+            tile = sb(name, [P, width], U8)
+            nc.gpsimd.memset(tile[:].bitcast(I32), 0)
             return tile
+
+        def load_scales(tile, src, queue, quadrants=range(4)):
+            for q in quadrants:
+                queue.dma_start(tile[32 * q : 32 * q + 4, :].bitcast(I32), src[0, 4 * q : 4 * q + 4, :].bitcast(I32))
 
         def load_column(name, src, queue):
             tile = sb(name, [P, PACK], F32)
             queue.dma_start(tile[:], src.rearrange("(p t) o -> p (t o)", t=PACK))
             return tile
 
-        xs = load_scales("xs", x_scales, nc.vector, nc.scalar)
-        w2s_raw = load_scales("w2s_raw", w2_scales, nc.vector, nc.scalar)
+        xs = zeroed_plane("xs", T)
+        w2s_raw = zeroed_plane("w2s_raw", H)
+        w1s_raw = zeroed_plane("w1s_raw", H)
+        w3s_raw = zeroed_plane("w3s_raw", H)
         two_l = load_list("two_l", two)
-        offs_l = load_list("offs_l", offs)
+        three_l = load_list("three_l", three)
+        load_scales(xs, x_scales, nc.scalar, (0, 1))
+        load_scales(xs, x_scales, nc.sync, (2, 3))
         xw = load_words("xw", x_words)
+        load_scales(w2s_raw, w2_scales, nc.scalar)
         w2w_raw = load_words("w2w_raw", w2_words)
         sl_c = load_column("sl_c", sl, nc.sync)
         th_c = load_column("th_c", th, nc.sync)
         n1_l = load_list("n1_l", n1)
-        w1s_raw = load_scales("w1s_raw", w1_scales, nc.gpsimd, nc.gpsimd)
+        offs_l = load_list("offs_l", offs)
+        load_scales(w1s_raw, w1_scales, nc.sync)
         w1w_raw = load_words("w1w_raw", w1_words)
         ga_c = load_column("ga_c", ga, nc.sync)
         n2_l = load_list("n2_l", n2)
-        three_l = load_list("three_l", three)
-        w3s_raw = load_scales("w3s_raw", w3_scales, nc.gpsimd, nc.gpsimd)
+        load_scales(w3s_raw, w3_scales, nc.sync)
         w3w_raw = load_words("w3w_raw", w3_words)
-        gb_c = load_column("gb_c", gb, nc.sync)
         tau_c = load_column("tau_c", tau, nc.sync)
         tau2_c = load_column("tau2_c", tau2, nc.sync)
+        gb_c = load_column("gb_c", gb, nc.sync)
         n3_l = load_list("n3_l", n3)
         n4_l = load_list("n4_l", n4)
         tau3_c = load_column("tau3_c", tau3, nc.sync)
@@ -84,9 +91,9 @@ def tile_picked_twkgxbedfegs_none_po_kernel(
             nc.vector.tensor_copy(tile[:], window[:].indirect(offsets[:]))
             return tile
 
-        def deal(name, raw, dtype, copy):
-            tile = sb(name, [P, H], dtype)
-            copy(tile[:].rearrange("p (t m) -> p m t", t=PACK), raw[:].rearrange("p (m t) -> p m t", t=PACK))
+        def deal_on_gpsimd(name, raw, dtype, tag=None):
+            tile = sb(name, [P, H], dtype, tag)
+            nc.gpsimd.tensor_copy(tile[:].rearrange("p (t m) -> p t m", t=PACK), raw[:].rearrange("p (m t) -> p t m", t=PACK))
             return tile
 
         def products(tag, words, scales, x_w, x_s):
@@ -102,20 +109,26 @@ def tile_picked_twkgxbedfegs_none_po_kernel(
             return banks
 
         x2s = gather("x2s", xs, two_l, U8)
-        w2w = deal("w2w", w2w_raw, U32, nc.scalar.copy)
-        x1s = gather("x1s", xs, offs_l, U8)
-        w2s = deal("w2s", w2s_raw, U8, nc.vector.tensor_copy)
-        x2w = gather("x2w", xw, two_l, U32, "w2s_raw")
+        w2w = sb("w2w", [P, H], U32)
+        for t in range(PACK):
+            nc.scalar.copy(w2w[:, t * P : (t + 1) * P], w2w_raw[:, t::PACK])
+        x3s = gather("x3s", xs, three_l, U8)
+        w2s = deal_on_gpsimd("w2s", w2s_raw, U8)
+        x2w = gather("x2w", xw, two_l, U32)
+        x3w = gather("x3w", xw, three_l, U32)
         sg_bias = sb("sg_bias", [P, PACK], F32)
         nc.vector.scalar_tensor_tensor(sg_bias[:], sl_c[:], -1.0, th_c[:], ALU.mult, ALU.mult)
         d_banks = products("pa", w2w, w2s, x2w, x2s)
 
-        w1w = deal("w1w", w1w_raw, U32, nc.scalar.copy)
-        w3w = deal("w3w", w3w_raw, U32, nc.scalar.copy)
+        w1s = deal_on_gpsimd("w1s", w1s_raw, U8)
+        w1w = deal_on_gpsimd("w1w", w1w_raw, U32)
+        w3s = deal_on_gpsimd("w3s", w3s_raw, U8)
+        w3w = deal_on_gpsimd("w3w", w3w_raw, U32)
 
         s_win = [sb("s_win%d" % t, [P, 1024], F32) for t in range(PACK)]
         sg = [s_win[t][:, V : V + S] for t in range(PACK)]
-        ea = [s_win[t][:, V + S :] for t in range(PACK)]
+        for t in range(PACK):
+            nc.gpsimd.memset(s_win[t][:, V + S :], 0.0)
         d_win = [sb("d_win%d" % t, [P, S], F32) for t in range(PACK)]
 
         def sigmoid_of(t):
@@ -125,52 +138,50 @@ def tile_picked_twkgxbedfegs_none_po_kernel(
                     ACT.Sigmoid, bias=sg_bias[:, t : t + 1], scale=sl_c[:, t : t + 1],
                 )
 
-        nc.vector.tensor_copy(d_win[0][:], d_banks[0][:])
-        sigmoid_of(0)
-        nc.vector.tensor_copy(d_win[1][:], d_banks[1][:])
-        sigmoid_of(1)
-        x1w = gather("x1w", xw, offs_l, U32)
-        w1s = deal("w1s", w1s_raw, U8, nc.vector.tensor_copy)
-        for t in (2, 3):
+        for t in range(PACK):
             nc.vector.tensor_copy(d_win[t][:], d_banks[t][:])
             sigmoid_of(t)
+        x1s = gather("x1s", xs, offs_l, U8, "x2s")
+        x1w = gather("x1w", xw, offs_l, U32, "x2w")
 
         y_banks = products("pb", w1w, w1s, x1w, x1s)
         y_win = [sb("y_win%d" % t, [P, S], F32) for t in range(PACK)]
         fetched = sb("fetched", [P, PACK, S], F32)
-        gated = sb("gated", [P, PACK, S], F32)
+        gated = sb("gated", [P, PACK, S], F32, "w3w_raw")
         for t in range(PACK):
             nc.vector.tensor_scalar(y_win[t][:], y_banks[t][:], ga_c[:, t : t + 1], None, ALU.mult)
             for h in range(2):
-                nc.scalar.activation(
-                    fetched[:, t, h * 256 : (h + 1) * 256], y_win[t][:].indirect(n2_l[:, h * 16 : (h + 1) * 16]), ACT.Copy, scale=-0.5,
-                )
+                looked_up = y_win[t][:].indirect(n2_l[:, h * 16 : (h + 1) * 16])
+                nc.scalar.activation(fetched[:, t, h * 256 : (h + 1) * 256], looked_up, ACT.Copy, scale=-0.5)
+            nc.gpsimd.tensor_tensor(gated[:, t, :], y_win[t][:], sg[t], ALU.mult)
 
-        x3s = gather("x3s", xs, three_l, U8)
-        x3w = gather("x3w", xw, three_l, U32)
-        w3s = deal("w3s", w3s_raw, U8, nc.vector.tensor_copy)
-        b_banks = products("pa", w3w, w3s, x3w, x3s)
+        b_banks = [psum.tile([P, 2, V], F32, name="b_bank%d" % j, tag="pa%d" % j) for j in range(2)]
+        for t in range(PACK):
+            rows = slice(t * P, (t + 1) * P)
+            nc.tensor.matmul_mx(
+                out=b_banks[t // 2][:, t % 2, :], lhsT=w3w[:, rows].bitcast(FP8X4), lhsT_scale=w3s[:, rows],
+                rhs=x3w[:].bitcast(FP8X4), rhs_scale=x3s[:], start=True, stop=True,
+            )
         gb15 = sb("gb15", [P, PACK], F32)
-        nc.vector.tensor_scalar(gb15[:], gb_c[:], 1.5, None, ALU.mult)
+        nc.gpsimd.tensor_scalar(gb15[:], gb_c[:], 1.5, 0.0, ALU.mult, ALU.add)
         neg_tau2 = sb("neg_tau2", [P, PACK], F32)
-        nc.vector.tensor_scalar(neg_tau2[:], tau2_c[:], -1.0, None, ALU.mult)
-        b_win = [sb("b_win%d" % t, [P, 2 * V], F32) for t in range(PACK)]
+        nc.gpsimd.tensor_scalar(neg_tau2[:], tau2_c[:], -1.0, 0.0, ALU.mult, ALU.add)
+        b_win = [sb("b_win%d" % t, [P, V], F32) for t in range(PACK)]
         top = sb("top", [P, PACK], F32)
         low = sb("low", [P, PACK], F32)
         weighted_b = sb("weighted_b", [P, PACK, V], F32)
         for t in range(PACK):
-            nc.vector.tensor_scalar(b_win[t][:, :V], b_banks[t][:], 1.0, None, ALU.mult, ALU.max, accum_out=top[:, t : t + 1])
-            nc.vector.tensor_scalar(b_win[t][:, V:], b_banks[t][:], 1.0, None, ALU.mult, ALU.min, accum_out=low[:, t : t + 1])
+            nc.vector.tensor_scalar(b_win[t][:], b_banks[t // 2][:, t % 2, :], 1.0, None, ALU.mult, ALU.max, accum_out=top[:, t : t + 1])
+        for j in range(2):
+            nc.vector.tensor_reduce(low[:, 2 * j : 2 * j + 2], b_banks[j][:], AXIS.X, ALU.min)
         ea_bias = sb("ea_bias", [P, PACK], F32)
         nc.vector.scalar_tensor_tensor(ea_bias[:], top[:], -1.0, tau_c[:], ALU.mult, ALU.mult)
         ea2_bias = sb("ea2_bias", [P, PACK], F32)
         nc.vector.tensor_tensor(ea2_bias[:], low[:], tau2_c[:], ALU.mult)
         for t in range(PACK):
-            nc.vector.tensor_scalar(weighted_b[:, t, :], b_win[t][:, V:], gb15[:, t : t + 1], None, ALU.mult)
+            nc.gpsimd.tensor_scalar(weighted_b[:, t, :], b_win[t][:], gb15[:, t : t + 1], 0.0, ALU.mult, ALU.add)
 
-        for t in range(PACK):
-            nc.vector.tensor_tensor(gated[:, t, :], y_win[t][:], sg[t], ALU.mult)
-        z_bf = sb("z_bf", [P, S * PACK], BF16)
+        z_bf = sb("z_bf", [P, S * PACK], BF16, "low")
         nc.vector.tensor_tensor(
             z_bf[:].rearrange("p (u m t) -> p m t u", u=PACK, t=PACK),
             gated[:].rearrange("p t (m u) -> p m t u", u=PACK),
@@ -181,28 +192,41 @@ def tile_picked_twkgxbedfegs_none_po_kernel(
         z_s = sb("z_s", [P, S], U8)
         nc.vector.quantize_mx(out=z_w[:].bitcast(FP8X4), scales=z_s[:], in_=z_bf[:])
 
+        HALF = V // 2
+        ea = sb("ea", [P, PACK, V], F32)
         ea2 = sb("ea2", [P, PACK, V], F32)
-        both = sb("both", [P, PACK, V], F32)
-        for t in range(PACK):
-            nc.scalar.activation(
-                ea[t], b_win[t][:].indirect(n3_l[:]), ACT.Exp, bias=ea_bias[:, t : t + 1], scale=tau_c[:, t : t + 1],
-            )
-            nc.scalar.activation(
-                ea2[:, t, :], b_win[t][:].indirect(n4_l[:]), ACT.Exp, bias=ea2_bias[:, t : t + 1], scale=neg_tau2[:, t : t + 1],
-            )
-            nc.vector.tensor_tensor(both[:, t, :], ea[t], ea2[:, t, :], ALU.add)
-        z2_bf = sb("z2_bf", [P, V * PACK], BF16)
-        nc.vector.tensor_tensor(
-            z2_bf[:].rearrange("p (c i t) -> p c t i", i=4, t=PACK),
-            both[:].rearrange("p t (c i) -> p c t i", i=4),
-            weighted_b[:].rearrange("p t (c i) -> p c t i", i=4),
-            ALU.mult,
-        )
         z2_w = sb("z2_w", [P, V], U32)
         z2_s = sb("z2_s", [P, V], U8)
-        nc.vector.quantize_mx(out=z2_w[:].bitcast(FP8X4), scales=z2_s[:], in_=z2_bf[:])
+        s_banks = [psum.tile([P, V], F32, name="s_bank%d" % t, tag="pb%d" % t) for t in range(PACK)]
+        for h in range(2):
+            cols = slice(h * HALF, (h + 1) * HALF)
+            entries = slice(h * HALF // 16, (h + 1) * HALF // 16)
+            both = sb("both%d" % h, [P, PACK, HALF], F32, "z2_ring%d" % h)
+            for t in range(PACK):
+                nc.scalar.activation(
+                    ea[:, t, cols], b_win[t][:].indirect(n3_l[:, entries]), ACT.Exp, bias=ea_bias[:, t : t + 1], scale=tau_c[:, t : t + 1],
+                )
+                nc.scalar.activation(
+                    ea2[:, t, cols], b_win[t][:].indirect(n4_l[:, entries]), ACT.Exp, bias=ea2_bias[:, t : t + 1], scale=neg_tau2[:, t : t + 1],
+                )
+                if t % 2:
+                    rows = slice(t - 1, t + 1)
+                    nc.vector.tensor_tensor(both[:, rows, :], ea[:, rows, cols], ea2[:, rows, cols], ALU.add)
+            z2_bf = sb("z2_bf%d" % h, [P, HALF * PACK], BF16, "z2_ring%d" % (1 - h))
+            nc.vector.tensor_tensor(
+                z2_bf[:].rearrange("p (c i t) -> p c t i", i=4, t=PACK),
+                both[:].rearrange("p t (c i) -> p c t i", i=4),
+                weighted_b[:, :, cols].rearrange("p t (c i) -> p c t i", i=4),
+                ALU.mult,
+            )
+            nc.vector.quantize_mx(out=z2_w[:, cols].bitcast(FP8X4), scales=z2_s[:, cols], in_=z2_bf[:])
+            for t in range(PACK):
+                rows = slice(t * P, (t + 1) * P)
+                nc.tensor.matmul_mx(
+                    out=s_banks[t][:, cols], lhsT=z_w[:, rows].bitcast(FP8X4), lhsT_scale=z_s[:, rows],
+                    rhs=z2_w[:, cols].bitcast(FP8X4), rhs_scale=z2_s[:, cols], start=True, stop=True,
+                )
 
-        s_banks = products("pb", z_w, z_s, z2_w, z2_s)
         top2 = sb("top2", [P, PACK], F32)
         ea3_bias = sb("ea3_bias", [P, PACK], F32)
         for t in range(PACK):
@@ -212,37 +236,37 @@ def tile_picked_twkgxbedfegs_none_po_kernel(
         out_rows = out_0.rearrange("(p t) v -> p t v", t=PACK)
         out_w = sb("out_w", [P, V], U32)
         out_s = sb("out_s", [P, V], U8)
-        CH = 128
-        for c in range(V // CH):
-            cols = slice(c * CH, (c + 1) * CH)
-            ea3 = sb("ea3_%d" % c, [P, PACK, CH, MEMBERS], F32)
-            pairs = sb("pairs_%d" % c, [P, PACK, CH, 2], F32)
-            den = sb("den_%d" % c, [P, PACK, CH], F32)
-            num = sb("num_%d" % c, [P, PACK, CH], F32)
-            for t in range(PACK):
-                nc.scalar.activation(
-                    ea3[:, t].rearrange("p v d -> p (v d)"),
-                    s_win[t][:].indirect(n5_l[:, c * CH // 4 : (c + 1) * CH // 4]),
-                    ACT.Exp, bias=ea3_bias[:, t : t + 1], scale=tau3_c[:, t : t + 1],
-                )
-                nc.vector.tensor_tensor(pairs[:, t], ea3[:, t, :, 0:2], ea3[:, t, :, 2:4], ALU.add)
-                nc.vector.scalar_tensor_tensor(den[:, t, :], pairs[:, t, :, 0], 0.5, pairs[:, t, :, 1], ALU.add, ALU.add)
-            prod2 = sb("prod2_%d" % c, [P, 2, CH], F32)
-            nc.vector.tensor_tensor(prod2[:], den[:, 0:2, :], den[:, 2:4, :], ALU.mult)
-            prod4 = sb("prod4_%d" % c, [P, CH], F32)
-            nc.vector.tensor_tensor(prod4[:], prod2[:, 0, :], prod2[:, 1, :], ALU.mult)
-            inv4 = sb("inv4_%d" % c, [P, CH], F32)
-            nc.vector.reciprocal(inv4[:], prod4[:])
-            for t in range(PACK):
-                nc.vector.tensor_tensor(num[:, t, :], s_win[t][:, cols], den[:, (t + 2) % PACK, :], ALU.mult)
-            inv2 = sb("inv2_%d" % c, [P, 2, CH], F32)
+        for start, width in ((0, 64), (64, 128), (192, 64)):
+            cols = slice(start, start + width)
+            entries = slice(start * MEMBERS // 16, (start + width) * MEMBERS // 16)
+            res = sb("res_%d" % start, [P, PACK, width], F32)
             for j in range(2):
-                nc.vector.scalar_tensor_tensor(inv2[:, j, :], inv4[:], 1.5, prod2[:, 1 - j, :], ALU.mult, ALU.mult)
-            res = sb("res_%d" % c, [P, PACK, CH], F32)
-            for j in range(2):
-                nc.vector.tensor_tensor(res[:, 2 * j : 2 * j + 2, :], num[:, 2 * j : 2 * j + 2, :], inv2[:], ALU.mult)
+                name = "_%d_%d" % (start, j)
+                ea3 = sb("ea3" + name, [P, 2, width * MEMBERS], F32)
+                for i in range(2):
+                    t = 2 * j + i
+                    nc.scalar.activation(
+                        ea3[:, i, :], s_win[t][:].indirect(n5_l[:, entries]),
+                        ACT.Exp, bias=ea3_bias[:, t : t + 1], scale=tau3_c[:, t : t + 1],
+                    )
+                members = ea3[:].rearrange("p i (v d) -> p (i v) d", d=MEMBERS)
+                pairs = sb("pairs" + name, [P, 2 * width, 2], F32)
+                (nc.vector if start + width == V and j == 1 else nc.gpsimd).tensor_tensor(pairs[:], members[:, :, 0:2], members[:, :, 2:4], ALU.add)
+                den = sb("den" + name, [P, 2, width], F32, "den")
+                for i in range(2):
+                    part = pairs[:, i * width : (i + 1) * width, :]
+                    nc.vector.scalar_tensor_tensor(den[:, i, :], part[:, :, 0], 0.5, part[:, :, 1], ALU.add, ALU.add)
+                num = sb("num" + name, [P, 2, width], F32)
+                nc.vector.tensor_tensor(num[:, 1, :], s_win[2 * j + 1][:, cols], den[:, 0, :], ALU.mult)
+                prod = sb("prod" + name, [P, width], F32)
+                nc.vector.tensor_tensor(prod[:], den[:, 0, :], den[:, 1, :], ALU.mult)
+                nc.vector.tensor_tensor(num[:, 0, :], s_win[2 * j][:, cols], den[:, 1, :], ALU.mult)
+                inv = sb("inv" + name, [P, width], F32)
+                nc.vector.reciprocal(inv[:], prod[:])
+                nc.vector.scalar_tensor_tensor(
+                    res[:, 2 * j : 2 * j + 2, :], num[:], 1.5, inv[:].unsqueeze(1).broadcast_to([P, 2, width]), ALU.mult, ALU.mult)
             nc.sync.dma_start(out_rows[:, :, cols], res[:])
-            res_bf = sb("res_bf_%d" % c, [P, CH * PACK], BF16)
+            res_bf = sb("res_bf_%d" % start, [P, width * PACK], BF16)
             nc.vector.tensor_copy(
                 res_bf[:].rearrange("p (c i t) -> p c t i", i=4, t=PACK),
                 res[:].rearrange("p t (c i) -> p c t i", i=4),

@@ -48,9 +48,9 @@ def tile_picked_twkgxbedfegs_none_po_kernel(
             nc.gpsimd.memset(tile[:].bitcast(I32), 0)
             return tile
 
-        def load_scales(tile, src, queue, quadrants=range(4)):
+        def load_scales(tile, src, queue, quadrants=range(4), row=0):
             for q in quadrants:
-                queue.dma_start(tile[32 * q : 32 * q + 4, :].bitcast(I32), src[0, 4 * q : 4 * q + 4, :].bitcast(I32))
+                queue.dma_start(tile[32 * q + row : 32 * q + row + 4, :].bitcast(I32), src[0, 4 * q : 4 * q + 4, :].bitcast(I32))
 
         def load_column(name, src, queue):
             tile = sb(name, [P, PACK], F32)
@@ -59,8 +59,7 @@ def tile_picked_twkgxbedfegs_none_po_kernel(
 
         xs = zeroed_plane("xs", T)
         w2s_raw = zeroed_plane("w2s_raw", H)
-        w1s_raw = zeroed_plane("w1s_raw", H)
-        w3s_raw = zeroed_plane("w3s_raw", H)
+        w13s_raw = zeroed_plane("w13s_raw", H)
         two_l = load_list("two_l", two)
         three_l = load_list("three_l", three)
         load_scales(xs, x_scales, nc.scalar, (0, 1))
@@ -68,16 +67,16 @@ def tile_picked_twkgxbedfegs_none_po_kernel(
         xw = load_words("xw", x_words)
         load_scales(w2s_raw, w2_scales, nc.scalar)
         w2w_raw = load_words("w2w_raw", w2_words)
-        sl_c = load_column("sl_c", sl, nc.sync)
-        th_c = load_column("th_c", th, nc.sync)
-        n1_l = load_list("n1_l", n1)
-        offs_l = load_list("offs_l", offs)
-        load_scales(w1s_raw, w1_scales, nc.sync)
+        sl_c = load_column("sl_c", sl, nc.gpsimd)
         w1w_raw = load_words("w1w_raw", w1_words)
+        w3w_raw = load_words("w3w_raw", w3_words)
+        th_c = load_column("th_c", th, nc.gpsimd)
+        offs_l = load_list("offs_l", offs)
+        n1_l = load_list("n1_l", n1)
+        load_scales(w13s_raw, w1_scales, nc.sync)
+        load_scales(w13s_raw, w3_scales, nc.sync, row=4)
         ga_c = load_column("ga_c", ga, nc.sync)
         n2_l = load_list("n2_l", n2)
-        load_scales(w3s_raw, w3_scales, nc.sync)
-        w3w_raw = load_words("w3w_raw", w3_words)
         tau_c = load_column("tau_c", tau, nc.sync)
         tau2_c = load_column("tau2_c", tau2, nc.sync)
         gb_c = load_column("gb_c", gb, nc.sync)
@@ -91,9 +90,9 @@ def tile_picked_twkgxbedfegs_none_po_kernel(
             nc.vector.tensor_copy(tile[:], window[:].indirect(offsets[:]))
             return tile
 
-        def deal_on_gpsimd(name, raw, dtype, tag=None):
-            tile = sb(name, [P, H], dtype, tag)
-            nc.gpsimd.tensor_copy(tile[:].rearrange("p (t m) -> p t m", t=PACK), raw[:].rearrange("p (m t) -> p t m", t=PACK))
+        def deal(name, raw, dtype, copy):
+            tile = sb(name, [P, H], dtype)
+            copy(tile[:].rearrange("p (t m) -> p m t", t=PACK), raw[:].rearrange("p (m t) -> p m t", t=PACK))
             return tile
 
         def products(tag, words, scales, x_w, x_s):
@@ -102,28 +101,31 @@ def tile_picked_twkgxbedfegs_none_po_kernel(
                 bank = psum.tile([P, x_w.shape[1]], F32, name="%s%d" % (tag, t), tag="%s%d" % (tag, t))
                 cols = slice(t * P, (t + 1) * P)
                 nc.tensor.matmul_mx(
-                    out=bank[:], lhsT=words[:, cols].bitcast(FP8X4), lhsT_scale=scales[:, cols],
+                    out=bank[:], lhsT=words[t].bitcast(FP8X4), lhsT_scale=scales[:, cols],
                     rhs=x_w[:].bitcast(FP8X4), rhs_scale=x_s[:], start=True, stop=True,
                 )
                 banks.append(bank)
             return banks
 
         x2s = gather("x2s", xs, two_l, U8)
-        w2w = sb("w2w", [P, H], U32)
-        for t in range(PACK):
-            nc.scalar.copy(w2w[:, t * P : (t + 1) * P], w2w_raw[:, t::PACK])
+        by_slot = w2w_raw[:].rearrange("p (m t) -> p m t", t=PACK)
+        w2w_first = sb("w2w_first", [P, P], U32)
+        nc.scalar.copy(w2w_first[:], by_slot[:, :, 0])
+        w2w_rest = sb("w2w_rest", [P, PACK - 1, P], U32)
+        nc.scalar.copy(w2w_rest[:].rearrange("p t m -> p m t"), by_slot[:, :, 1:])
+        w2w = [w2w_first[:]] + [w2w_rest[:, t, :] for t in range(PACK - 1)]
         x3s = gather("x3s", xs, three_l, U8)
-        w2s = deal_on_gpsimd("w2s", w2s_raw, U8)
+        w2s = deal("w2s", w2s_raw, U8, nc.vector.tensor_copy)
         x2w = gather("x2w", xw, two_l, U32)
         x3w = gather("x3w", xw, three_l, U32)
         sg_bias = sb("sg_bias", [P, PACK], F32)
-        nc.vector.scalar_tensor_tensor(sg_bias[:], sl_c[:], -1.0, th_c[:], ALU.mult, ALU.mult)
+        neg_th = sb("neg_th", [P, PACK], F32)
+        nc.gpsimd.tensor_scalar(neg_th[:], th_c[:], -1.0, 0.0, ALU.mult, ALU.add)
+        nc.gpsimd.tensor_tensor(sg_bias[:], sl_c[:], neg_th[:], ALU.mult)
         d_banks = products("pa", w2w, w2s, x2w, x2s)
 
-        w1s = deal_on_gpsimd("w1s", w1s_raw, U8)
-        w1w = deal_on_gpsimd("w1w", w1w_raw, U32)
-        w3s = deal_on_gpsimd("w3s", w3s_raw, U8)
-        w3w = deal_on_gpsimd("w3w", w3w_raw, U32)
+        w1w = deal("w1w", w1w_raw, U32, nc.scalar.copy)
+        w3w = deal("w3w", w3w_raw, U32, nc.scalar.copy)
 
         s_win = [sb("s_win%d" % t, [P, 1024], F32) for t in range(PACK)]
         sg = [s_win[t][:, V : V + S] for t in range(PACK)]
@@ -138,16 +140,21 @@ def tile_picked_twkgxbedfegs_none_po_kernel(
                     ACT.Sigmoid, bias=sg_bias[:, t : t + 1], scale=sl_c[:, t : t + 1],
                 )
 
-        for t in range(PACK):
+        nc.scalar.copy(d_win[0][:], d_banks[0][:])
+        sigmoid_of(0)
+        x1s = gather("x1s", xs, offs_l, U8, "w2w_first")
+        for t in (1, 2):
             nc.vector.tensor_copy(d_win[t][:], d_banks[t][:])
             sigmoid_of(t)
-        x1s = gather("x1s", xs, offs_l, U8, "x2s")
         x1w = gather("x1w", xw, offs_l, U32, "x2w")
+        nc.vector.tensor_copy(d_win[3][:], d_banks[3][:])
+        sigmoid_of(3)
+        w13s = deal("w13s", w13s_raw, U8, nc.vector.tensor_copy)
 
-        y_banks = products("pb", w1w, w1s, x1w, x1s)
+        y_banks = products("pb", [w1w[:, t * P : (t + 1) * P] for t in range(PACK)], w13s, x1w, x1s)
         y_win = [sb("y_win%d" % t, [P, S], F32) for t in range(PACK)]
         fetched = sb("fetched", [P, PACK, S], F32)
-        gated = sb("gated", [P, PACK, S], F32, "w3w_raw")
+        gated = sb("gated", [P, PACK, S], F32)
         for t in range(PACK):
             nc.vector.tensor_scalar(y_win[t][:], y_banks[t][:], ga_c[:, t : t + 1], None, ALU.mult)
             for h in range(2):
@@ -159,13 +166,13 @@ def tile_picked_twkgxbedfegs_none_po_kernel(
         for t in range(PACK):
             rows = slice(t * P, (t + 1) * P)
             nc.tensor.matmul_mx(
-                out=b_banks[t // 2][:, t % 2, :], lhsT=w3w[:, rows].bitcast(FP8X4), lhsT_scale=w3s[:, rows],
+                out=b_banks[t // 2][:, t % 2, :], lhsT=w3w[:, rows].bitcast(FP8X4), lhsT_scale=w13s[4:, rows],
                 rhs=x3w[:].bitcast(FP8X4), rhs_scale=x3s[:], start=True, stop=True,
             )
         gb15 = sb("gb15", [P, PACK], F32)
-        nc.gpsimd.tensor_scalar(gb15[:], gb_c[:], 1.5, 0.0, ALU.mult, ALU.add)
+        nc.scalar.activation(gb15[:], gb_c[:], ACT.Copy, scale=1.5)
         neg_tau2 = sb("neg_tau2", [P, PACK], F32)
-        nc.gpsimd.tensor_scalar(neg_tau2[:], tau2_c[:], -1.0, 0.0, ALU.mult, ALU.add)
+        nc.scalar.activation(neg_tau2[:], tau2_c[:], ACT.Copy, scale=-1.0)
         b_win = [sb("b_win%d" % t, [P, V], F32) for t in range(PACK)]
         top = sb("top", [P, PACK], F32)
         low = sb("low", [P, PACK], F32)
@@ -179,7 +186,7 @@ def tile_picked_twkgxbedfegs_none_po_kernel(
         ea2_bias = sb("ea2_bias", [P, PACK], F32)
         nc.vector.tensor_tensor(ea2_bias[:], low[:], tau2_c[:], ALU.mult)
         for t in range(PACK):
-            nc.gpsimd.tensor_scalar(weighted_b[:, t, :], b_win[t][:], gb15[:, t : t + 1], 0.0, ALU.mult, ALU.add)
+            nc.vector.tensor_scalar(weighted_b[:, t, :], b_win[t][:], gb15[:, t : t + 1], None, ALU.mult)
 
         z_bf = sb("z_bf", [P, S * PACK], BF16, "low")
         nc.vector.tensor_tensor(
@@ -197,7 +204,7 @@ def tile_picked_twkgxbedfegs_none_po_kernel(
         ea2 = sb("ea2", [P, PACK, V], F32)
         z2_w = sb("z2_w", [P, V], U32)
         z2_s = sb("z2_s", [P, V], U8)
-        s_banks = [psum.tile([P, V], F32, name="s_bank%d" % t, tag="pb%d" % t) for t in range(PACK)]
+        s_banks = [psum.tile([P, 2, V], F32, name="s_bank%d" % j, tag="pb%d" % j) for j in range(2)]
         for h in range(2):
             cols = slice(h * HALF, (h + 1) * HALF)
             entries = slice(h * HALF // 16, (h + 1) * HALF // 16)
@@ -223,51 +230,60 @@ def tile_picked_twkgxbedfegs_none_po_kernel(
             for t in range(PACK):
                 rows = slice(t * P, (t + 1) * P)
                 nc.tensor.matmul_mx(
-                    out=s_banks[t][:, cols], lhsT=z_w[:, rows].bitcast(FP8X4), lhsT_scale=z_s[:, rows],
+                    out=s_banks[t // 2][:, t % 2, cols], lhsT=z_w[:, rows].bitcast(FP8X4), lhsT_scale=z_s[:, rows],
                     rhs=z2_w[:, cols].bitcast(FP8X4), rhs_scale=z2_s[:, cols], start=True, stop=True,
                 )
 
         top2 = sb("top2", [P, PACK], F32)
         ea3_bias = sb("ea3_bias", [P, PACK], F32)
         for t in range(PACK):
-            nc.vector.tensor_scalar(s_win[t][:, :V], s_banks[t][:], 0.0625, None, ALU.mult, ALU.max, accum_out=top2[:, t : t + 1])
+            nc.vector.tensor_scalar(s_win[t][:, :V], s_banks[t // 2][:, t % 2, :], 0.0625, None, ALU.mult, ALU.max, accum_out=top2[:, t : t + 1])
             nc.vector.scalar_tensor_tensor(ea3_bias[:, t : t + 1], top2[:, t : t + 1], -1.0, tau3_c[:, t : t + 1], ALU.mult, ALU.mult)
 
         out_rows = out_0.rearrange("(p t) v -> p t v", t=PACK)
         out_w = sb("out_w", [P, V], U32)
         out_s = sb("out_s", [P, V], U8)
-        for start, width in ((0, 64), (64, 128), (192, 64)):
+        GROUP_STARTS = (0, 2, 3)
+        RINGS = {0: "ring_prod4", 2: "ring_inv2", 3: "ring_num"}
+        for start, width in ((0, 128), (128, 128)):
             cols = slice(start, start + width)
             entries = slice(start * MEMBERS // 16, (start + width) * MEMBERS // 16)
-            res = sb("res_%d" % start, [P, PACK, width], F32)
+            name = "_%d" % start
+            ea3 = sb("ea3" + name, [P, PACK, width, MEMBERS], F32)
+            den = sb("den" + name, [P, PACK, width], F32)
+            for t in range(PACK):
+                nc.scalar.activation(
+                    ea3[:, t].rearrange("p v d -> p (v d)"), s_win[t][:].indirect(n5_l[:, entries]),
+                    ACT.Exp, bias=ea3_bias[:, t : t + 1], scale=tau3_c[:, t : t + 1],
+                )
+                if t in GROUP_STARTS:
+                    first = t
+                if t + 1 in GROUP_STARTS or t + 1 == PACK:
+                    rows = slice(first, t + 1)
+                    members = ea3[:, rows].rearrange("p t v d -> p (t v) d")
+                    halves = sb("pairs%s_%d" % (name, first), [P, (t + 1 - first) * width, 2], F32, RINGS[first])[:]
+                    nc.vector.tensor_tensor(halves, members[:, :, 0:2], members[:, :, 2:4], ALU.add)
+                    nc.vector.scalar_tensor_tensor(
+                        den[:, rows, :].rearrange("p t v -> p (t v)"), halves[:, :, 0], 0.5, halves[:, :, 1], ALU.add, ALU.add)
+            prod2 = sb("prod2" + name, [P, 2, width], F32)
+            nc.vector.tensor_tensor(prod2[:], den[:, 0:2, :], den[:, 2:4, :], ALU.mult)
+            prod4 = sb("prod4" + name, [P, width], F32, "ring_prod4")
+            nc.vector.tensor_tensor(prod4[:], prod2[:, 0, :], prod2[:, 1, :], ALU.mult)
+            inv4 = sb("inv4" + name, [P, width], F32)
+            nc.vector.reciprocal(inv4[:], prod4[:])
+            num = sb("num" + name, [P, PACK, width], F32, "ring_num")
             for j in range(2):
-                name = "_%d_%d" % (start, j)
-                ea3 = sb("ea3" + name, [P, 2, width * MEMBERS], F32)
-                for i in range(2):
-                    t = 2 * j + i
-                    nc.scalar.activation(
-                        ea3[:, i, :], s_win[t][:].indirect(n5_l[:, entries]),
-                        ACT.Exp, bias=ea3_bias[:, t : t + 1], scale=tau3_c[:, t : t + 1],
-                    )
-                members = ea3[:].rearrange("p i (v d) -> p (i v) d", d=MEMBERS)
-                pairs = sb("pairs" + name, [P, 2 * width, 2], F32)
-                (nc.vector if start + width == V and j == 1 else nc.gpsimd).tensor_tensor(pairs[:], members[:, :, 0:2], members[:, :, 2:4], ALU.add)
-                den = sb("den" + name, [P, 2, width], F32, "den")
-                for i in range(2):
-                    part = pairs[:, i * width : (i + 1) * width, :]
-                    nc.vector.scalar_tensor_tensor(den[:, i, :], part[:, :, 0], 0.5, part[:, :, 1], ALU.add, ALU.add)
-                num = sb("num" + name, [P, 2, width], F32)
-                nc.vector.tensor_tensor(num[:, 1, :], s_win[2 * j + 1][:, cols], den[:, 0, :], ALU.mult)
-                prod = sb("prod" + name, [P, width], F32)
-                nc.vector.tensor_tensor(prod[:], den[:, 0, :], den[:, 1, :], ALU.mult)
-                nc.vector.tensor_tensor(num[:, 0, :], s_win[2 * j][:, cols], den[:, 1, :], ALU.mult)
-                inv = sb("inv" + name, [P, width], F32)
-                nc.vector.reciprocal(inv[:], prod[:])
-                nc.vector.scalar_tensor_tensor(
-                    res[:, 2 * j : 2 * j + 2, :], num[:], 1.5, inv[:].unsqueeze(1).broadcast_to([P, 2, width]), ALU.mult, ALU.mult)
+                nc.vector.tensor_tensor(num[:, 2 * j : 2 * j + 2, :], s_banks[j][:, :, cols], den[:, 2 - 2 * j : 4 - 2 * j, :], ALU.mult)
+            inv2 = sb("inv2" + name, [P, 2, width], F32, "ring_inv2")
+            for j in range(2):
+                nc.vector.scalar_tensor_tensor(inv2[:, j, :], inv4[:], 1.5 * 0.0625, prod2[:, 1 - j, :], ALU.mult, ALU.mult)
+            res = sb("res" + name, [P, PACK, width], F32)
+            nc.vector.tensor_tensor(
+                res[:].rearrange("p (j t) v -> p j (t v)", j=2), num[:].rearrange("p (j t) v -> p j (t v)", j=2),
+                inv2[:].rearrange("p t v -> p (t v)").unsqueeze(1).broadcast_to([P, 2, 2 * width]), ALU.mult)
             nc.sync.dma_start(out_rows[:, :, cols], res[:])
-            res_bf = sb("res_bf_%d" % start, [P, width * PACK], BF16)
-            nc.vector.tensor_copy(
+            res_bf = sb("res_bf" + name, [P, width * PACK], BF16)
+            (nc.vector.tensor_copy if start + width == V else nc.scalar.copy)(
                 res_bf[:].rearrange("p (c i t) -> p c t i", i=4, t=PACK),
                 res[:].rearrange("p t (c i) -> p c t i", i=4),
             )

from contextlib import ExitStack

import concourse.mybir as mybir

F32 = mybir.dt.float32
BF16 = mybir.dt.bfloat16
U32 = mybir.dt.uint32
I32 = mybir.dt.int32
U16 = mybir.dt.uint16
U8 = mybir.dt.uint8
FP8X4 = mybir.dt.float8_e4m3fn_x4
ALU = mybir.AluOpType
ACT = mybir.ActivationFunctionType
AXIS = mybir.AxisListType

P = 128
PACK = 4
T, S, V, H = 2048, 512, 256, 512
MEMBERS = 4
FLOPS = 2 * 512 * (H * S + H * S + H * V + S * V)


def tile_picked_twkgxbedfegs_none_po_kernel(
    tc, x_words, x_scales, w1_words, w1_scales, w2_words, w2_scales, sl, th, w3_words, w3_scales,
    tau, tau2, ga, gb, tau3, offs, two, n1, n2, three, n3, n4, n5, out_0, out_1, out_2,
):
    nc = tc.nc
    with ExitStack() as ctx:
        lists = ctx.enter_context(tc.tile_pool(name="lists", bufs=1))
        keep = ctx.enter_context(tc.tile_pool(name="keep", bufs=1))
        psum = ctx.enter_context(tc.psum_pool(name="psum", bufs=1))

        def sb(name, shape, dtype, tag=None):
            return keep.tile(shape, dtype, name=name, tag=tag or name, align_bytes=64)

        def load_list(name, src):
            tile = lists.tile(list(src.shape), U16, name=name)
            nc.sync.dma_start(tile[:], src)
            return tile

        def load_words(name, src, queue=nc.sync):
            tile = sb(name, [P, src.shape[2]], U32)
            queue.dma_start(tile[:].bitcast(I32), src[0].rearrange("p c r -> p (c r)").bitcast(I32))
            return tile

        def zeroed_plane(name, width):
            tile = sb(name, [P, width], U8)
            nc.gpsimd.memset(tile[:].bitcast(I32), 0)
            return tile

        def load_scales(tile, src, queue, quadrants=range(4), row=0):
            for q in quadrants:
                queue.dma_start(tile[32 * q + row : 32 * q + row + 4, :].bitcast(I32), src[0, 4 * q : 4 * q + 4, :].bitcast(I32))

        def load_column(name, src, queue):
            tile = sb(name, [P, PACK], F32)
            queue.dma_start(tile[:], src.rearrange("(p t) o -> p (t o)", t=PACK))
            return tile

        xs = zeroed_plane("xs", T)
        w2s_raw = zeroed_plane("w2s_raw", H)
        w13s_raw = zeroed_plane("w13s_raw", H)
        two_l = load_list("two_l", two)
        three_l = load_list("three_l", three)
        load_scales(xs, x_scales, nc.scalar, (0, 1))
        load_scales(xs, x_scales, nc.sync, (2, 3))
        xw = load_words("xw", x_words)
        load_scales(w2s_raw, w2_scales, nc.scalar)
        w2w_raw = load_words("w2w_raw", w2_words)
        sl_c = load_column("sl_c", sl, nc.gpsimd)
        w1w_raw = load_words("w1w_raw", w1_words)
        w3w_raw = load_words("w3w_raw", w3_words)
        th_c = load_column("th_c", th, nc.gpsimd)
        offs_l = load_list("offs_l", offs)
        n1_l = load_list("n1_l", n1)
        load_scales(w13s_raw, w1_scales, nc.sync)
        load_scales(w13s_raw, w3_scales, nc.sync, row=4)
        ga_c = load_column("ga_c", ga, nc.sync)
        n2_l = load_list("n2_l", n2)
        tau_c = load_column("tau_c", tau, nc.sync)
        tau2_c = load_column("tau2_c", tau2, nc.sync)
        gb_c = load_column("gb_c", gb, nc.sync)
        n3_l = load_list("n3_l", n3)
        n4_l = load_list("n4_l", n4)
        tau3_c = load_column("tau3_c", tau3, nc.sync)
        n5_l = load_list("n5_l", n5)

        def gather(name, window, offsets, dtype, tag=None):
            tile = sb(name, [P, offsets.shape[1] * 16], dtype, tag)
            nc.vector.tensor_copy(tile[:], window[:].indirect(offsets[:]))
            return tile

        def deal(name, raw, dtype, copy):
            tile = sb(name, [P, H], dtype)
            copy(tile[:].rearrange("p (t m) -> p m t", t=PACK), raw[:].rearrange("p (m t) -> p m t", t=PACK))
            return tile

        def products(tag, words, scales, x_w, x_s):
            banks = []
            for t in range(PACK):
                bank = psum.tile([P, x_w.shape[1]], F32, name="%s%d" % (tag, t), tag="%s%d" % (tag, t))
                cols = slice(t * P, (t + 1) * P)
                nc.tensor.matmul_mx(
                    out=bank[:], lhsT=words[t].bitcast(FP8X4), lhsT_scale=scales[:, cols],
                    rhs=x_w[:].bitcast(FP8X4), rhs_scale=x_s[:], start=True, stop=True,
                )
                banks.append(bank)
            return banks

        x2s = gather("x2s", xs, two_l, U8)
        by_slot = w2w_raw[:].rearrange("p (m t) -> p m t", t=PACK)
        w2w_first = sb("w2w_first", [P, P], U32)
        nc.scalar.copy(w2w_first[:], by_slot[:, :, 0])
        w2w_rest = sb("w2w_rest", [P, PACK - 1, P], U32)
        nc.scalar.copy(w2w_rest[:].rearrange("p t m -> p m t"), by_slot[:, :, 1:])
        w2w = [w2w_first[:]] + [w2w_rest[:, t, :] for t in range(PACK - 1)]
        x3s = gather("x3s", xs, three_l, U8)
        w2s = deal("w2s", w2s_raw, U8, nc.vector.tensor_copy)
        x2w = gather("x2w", xw, two_l, U32)
        x3w = gather("x3w", xw, three_l, U32)
        sg_bias = sb("sg_bias", [P, PACK], F32)
        neg_th = sb("neg_th", [P, PACK], F32)
        nc.gpsimd.tensor_scalar(neg_th[:], th_c[:], -1.0, 0.0, ALU.mult, ALU.add)
        nc.gpsimd.tensor_tensor(sg_bias[:], sl_c[:], neg_th[:], ALU.mult)
        d_banks = products("pa", w2w, w2s, x2w, x2s)

        w1w = deal("w1w", w1w_raw, U32, nc.scalar.copy)
        w3w = deal("w3w", w3w_raw, U32, nc.scalar.copy)

        s_win = [sb("s_win%d" % t, [P, 1024], F32) for t in range(PACK)]
        sg = [s_win[t][:, V : V + S] for t in range(PACK)]
        for t in range(PACK):
            nc.gpsimd.memset(s_win[t][:, V + S :], 0.0)
        d_win = [sb("d_win%d" % t, [P, S], F32) for t in range(PACK)]

        def sigmoid_of(t):
            for h in range(2):
                nc.scalar.activation(
                    sg[t][:, h * 256 : (h + 1) * 256], d_win[t][:].indirect(n1_l[:, h * 16 : (h + 1) * 16]),
                    ACT.Sigmoid, bias=sg_bias[:, t : t + 1], scale=sl_c[:, t : t + 1],
                )

        nc.scalar.copy(d_win[0][:], d_banks[0][:])
        sigmoid_of(0)
        x1s = gather("x1s", xs, offs_l, U8, "w2w_first")
        for t in (1, 2):
            nc.vector.tensor_copy(d_win[t][:], d_banks[t][:])
            sigmoid_of(t)
        x1w = gather("x1w", xw, offs_l, U32, "x2w")
        nc.vector.tensor_copy(d_win[3][:], d_banks[3][:])
        sigmoid_of(3)
        w13s = deal("w13s", w13s_raw, U8, nc.vector.tensor_copy)

        y_banks = products("pb", [w1w[:, t * P : (t + 1) * P] for t in range(PACK)], w13s, x1w, x1s)
        y_win = [sb("y_win%d" % t, [P, S], F32) for t in range(PACK)]
        fetched = sb("fetched", [P, PACK, S], F32)
        gated = sb("gated", [P, PACK, S], F32)
        for t in range(PACK):
            nc.vector.tensor_scalar(y_win[t][:], y_banks[t][:], ga_c[:, t : t + 1], None, ALU.mult)
            for h in range(2):
                looked_up = y_win[t][:].indirect(n2_l[:, h * 16 : (h + 1) * 16])
                nc.scalar.activation(fetched[:, t, h * 256 : (h + 1) * 256], looked_up, ACT.Copy, scale=-0.5)
            nc.gpsimd.tensor_tensor(gated[:, t, :], y_win[t][:], sg[t], ALU.mult)

        b_banks = [psum.tile([P, 2, V], F32, name="b_bank%d" % j, tag="pa%d" % j) for j in range(2)]
        for t in range(PACK):
            rows = slice(t * P, (t + 1) * P)
            nc.tensor.matmul_mx(
                out=b_banks[t // 2][:, t % 2, :], lhsT=w3w[:, rows].bitcast(FP8X4), lhsT_scale=w13s[4:, rows],
                rhs=x3w[:].bitcast(FP8X4), rhs_scale=x3s[:], start=True, stop=True,
            )
        gb15 = sb("gb15", [P, PACK], F32)
        nc.scalar.activation(gb15[:], gb_c[:], ACT.Copy, scale=1.5)
        neg_tau2 = sb("neg_tau2", [P, PACK], F32)
        nc.scalar.activation(neg_tau2[:], tau2_c[:], ACT.Copy, scale=-1.0)
        b_win = [sb("b_win%d" % t, [P, V], F32) for t in range(PACK)]
        top = sb("top", [P, PACK], F32)
        low = sb("low", [P, PACK], F32)
        weighted_b = sb("weighted_b", [P, PACK, V], F32)
        for t in range(PACK):
            nc.vector.tensor_scalar(b_win[t][:], b_banks[t // 2][:, t % 2, :], 1.0, None, ALU.mult, ALU.max, accum_out=top[:, t : t + 1])
        for j in range(2):
            nc.vector.tensor_reduce(low[:, 2 * j : 2 * j + 2], b_banks[j][:], AXIS.X, ALU.min)
        ea_bias = sb("ea_bias", [P, PACK], F32)
        nc.vector.scalar_tensor_tensor(ea_bias[:], top[:], -1.0, tau_c[:], ALU.mult, ALU.mult)
        ea2_bias = sb("ea2_bias", [P, PACK], F32)
        nc.vector.tensor_tensor(ea2_bias[:], low[:], tau2_c[:], ALU.mult)
        for t in range(PACK):
            nc.vector.tensor_scalar(weighted_b[:, t, :], b_win[t][:], gb15[:, t : t + 1], None, ALU.mult)

        z_bf = sb("z_bf", [P, S * PACK], BF16, "low")
        nc.vector.tensor_tensor(
            z_bf[:].rearrange("p (u m t) -> p m t u", u=PACK, t=PACK),
            gated[:].rearrange("p t (m u) -> p m t u", u=PACK),
            fetched[:].rearrange("p t (m u) -> p m t u", u=PACK),
            ALU.add,
        )
        z_w = sb("z_w", [P, S], U32)
        z_s = sb("z_s", [P, S], U8)
        nc.vector.quantize_mx(out=z_w[:].bitcast(FP8X4), scales=z_s[:], in_=z_bf[:])

        HALF = V // 2
        ea = sb("ea", [P, PACK, V], F32)
        ea2 = sb("ea2", [P, PACK, V], F32)
        z2_w = sb("z2_w", [P, V], U32)
        z2_s = sb("z2_s", [P, V], U8)
        s_banks = [psum.tile([P, 2, V], F32, name="s_bank%d" % j, tag="pb%d" % j) for j in range(2)]
        for h in range(2):
            cols = slice(h * HALF, (h + 1) * HALF)
            entries = slice(h * HALF // 16, (h + 1) * HALF // 16)
            both = sb("both%d" % h, [P, PACK, HALF], F32, "z2_ring%d" % h)
            for t in range(PACK):
                nc.scalar.activation(
                    ea[:, t, cols], b_win[t][:].indirect(n3_l[:, entries]), ACT.Exp, bias=ea_bias[:, t : t + 1], scale=tau_c[:, t : t + 1],
                )
                nc.scalar.activation(
                    ea2[:, t, cols], b_win[t][:].indirect(n4_l[:, entries]), ACT.Exp, bias=ea2_bias[:, t : t + 1], scale=neg_tau2[:, t : t + 1],
                )
                if t % 2:
                    rows = slice(t - 1, t + 1)
                    nc.vector.tensor_tensor(both[:, rows, :], ea[:, rows, cols], ea2[:, rows, cols], ALU.add)
            z2_bf = sb("z2_bf%d" % h, [P, HALF * PACK], BF16, "z2_ring%d" % (1 - h))
            nc.vector.tensor_tensor(
                z2_bf[:].rearrange("p (c i t) -> p c t i", i=4, t=PACK),
                both[:].rearrange("p t (c i) -> p c t i", i=4),
                weighted_b[:, :, cols].rearrange("p t (c i) -> p c t i", i=4),
                ALU.mult,
            )
            nc.vector.quantize_mx(out=z2_w[:, cols].bitcast(FP8X4), scales=z2_s[:, cols], in_=z2_bf[:])
            for t in range(PACK):
                rows = slice(t * P, (t + 1) * P)
                nc.tensor.matmul_mx(
                    out=s_banks[t // 2][:, t % 2, cols], lhsT=z_w[:, rows].bitcast(FP8X4), lhsT_scale=z_s[:, rows],
                    rhs=z2_w[:, cols].bitcast(FP8X4), rhs_scale=z2_s[:, cols], start=True, stop=True,
                )

        top2 = sb("top2", [P, PACK], F32)
        ea3_bias = sb("ea3_bias", [P, PACK], F32)
        for t in range(PACK):
            nc.vector.tensor_scalar(s_win[t][:, :V], s_banks[t // 2][:, t % 2, :], 0.0625, None, ALU.mult, ALU.max, accum_out=top2[:, t : t + 1])
            nc.vector.scalar_tensor_tensor(ea3_bias[:, t : t + 1], top2[:, t : t + 1], -1.0, tau3_c[:, t : t + 1], ALU.mult, ALU.mult)

        out_rows = out_0.rearrange("(p t) v -> p t v", t=PACK)
        out_w = sb("out_w", [P, V], U32)
        out_s = sb("out_s", [P, V], U8)
        GROUP_STARTS = (0, 2, 3)
        RINGS = {0: "ring_prod4", 2: "ring_inv2", 3: "ring_num"}
        for start, width in ((0, 128), (128, 128)):
            cols = slice(start, start + width)
            entries = slice(start * MEMBERS // 16, (start + width) * MEMBERS // 16)
            name = "_%d" % start
            ea3 = sb("ea3" + name, [P, PACK, width, MEMBERS], F32)
            den = sb("den" + name, [P, PACK, width], F32)
            for t in range(PACK):
                nc.scalar.activation(
                    ea3[:, t].rearrange("p v d -> p (v d)"), s_win[t][:].indirect(n5_l[:, entries]),
                    ACT.Exp, bias=ea3_bias[:, t : t + 1], scale=tau3_c[:, t : t + 1],
                )
                if t in GROUP_STARTS:
                    first = t
                if t + 1 in GROUP_STARTS or t + 1 == PACK:
                    rows = slice(first, t + 1)
                    members = ea3[:, rows].rearrange("p t v d -> p (t v) d")
                    halves = sb("pairs%s_%d" % (name, first), [P, (t + 1 - first) * width, 2], F32, RINGS[first])[:]
                    nc.vector.tensor_tensor(halves, members[:, :, 0:2], members[:, :, 2:4], ALU.add)
                    nc.vector.scalar_tensor_tensor(
                        den[:, rows, :].rearrange("p t v -> p (t v)"), halves[:, :, 0], 0.5, halves[:, :, 1], ALU.add, ALU.add)
            prod2 = sb("prod2" + name, [P, 2, width], F32)
            nc.vector.tensor_tensor(prod2[:], den[:, 0:2, :], den[:, 2:4, :], ALU.mult)
            prod4 = sb("prod4" + name, [P, width], F32, "ring_prod4")
            nc.vector.tensor_tensor(prod4[:], prod2[:, 0, :], prod2[:, 1, :], ALU.mult)
            inv4 = sb("inv4" + name, [P, width], F32)
            nc.vector.reciprocal(inv4[:], prod4[:])
            num = sb("num" + name, [P, PACK, width], F32, "ring_num")
            for j in range(2):
                nc.vector.tensor_tensor(num[:, 2 * j : 2 * j + 2, :], s_banks[j][:, :, cols], den[:, 2 - 2 * j : 4 - 2 * j, :], ALU.mult)
            inv2 = sb("inv2" + name, [P, 2, width], F32, "ring_inv2")
            for j in range(2):
                nc.vector.scalar_tensor_tensor(inv2[:, j, :], inv4[:], 1.5 * 0.0625, prod2[:, 1 - j, :], ALU.mult, ALU.mult)
            res = sb("res" + name, [P, PACK, width], F32)
            nc.vector.tensor_tensor(
                res[:].rearrange("p (j t) v -> p j (t v)", j=2), num[:].rearrange("p (j t) v -> p j (t v)", j=2),
                inv2[:].rearrange("p t v -> p (t v)").unsqueeze(1).broadcast_to([P, 2, 2 * width]), ALU.mult)
            nc.sync.dma_start(out_rows[:, :, cols], res[:])
            res_bf = sb("res_bf" + name, [P, width * PACK], BF16)
            (nc.vector.tensor_copy if start + width == V else nc.scalar.copy)(
                res_bf[:].rearrange("p (c i t) -> p c t i", i=4, t=PACK),
                res[:].rearrange("p t (c i) -> p c t i", i=4),
            )
            nc.vector.quantize_mx(out=out_w[:, cols].bitcast(FP8X4), scales=out_s[:, cols], in_=res_bf[:])
        nc.sync.dma_start(out_1[0].rearrange("p c r -> p (c r)").bitcast(I32), out_w[:].bitcast(I32))
        for q in range(4):
            queue = nc.scalar if q % 2 else nc.sync
            queue.dma_start(out_2[0, 4 * q : 4 * q + 4, :].bitcast(I32), out_s[32 * q : 32 * q + 4, :].bitcast(I32))
